import numpy as np, ml_dtypes
CORES = [9,25,41,57]
N = 4
import mx_ref
BF = ml_dtypes.bfloat16
def gcols(t, e):
    v = np.concatenate([t.reshape(8, 16, -1, 4), np.zeros((8, 16, 1, 4), BF)], axis=2)
    return np.ascontiguousarray(np.stack([v[g][:, e[g]] for g in range(8)])).reshape(128, -1)
def tile(rs):
    return np.stack(rs, axis=2).reshape(128, -1).astype(BF)
def pick(q, e):
    c = np.concatenate([q[0].reshape(128, -1, 4), np.zeros((128, 1, 4), np.uint8)], axis=1); s = np.concatenate([q[1], np.ones((16, 1), np.uint8)], axis=1)
    return (np.ascontiguousarray(c[:, e].reshape(128, -1)), np.ascontiguousarray(s[:, e]))
def join(*qs):
    return (np.concatenate([q[0] for q in qs], axis=1), np.concatenate([q[1] for q in qs], axis=1))
def put(q, e, v):
    c, s = q[0].reshape(128, -1, 4).copy(), q[1].copy(); c[:, e] = v[0].reshape(128, -1, 4); s[:, e] = v[1]
    return (c.reshape(128, -1), s)
def pk(c, s):
    return (np.ascontiguousarray(c), mx_ref.live(s))
def emit(q):
    return q[0], q[1]
def packed(v, rng):
    q = [mx_ref.quantize(np.ascontiguousarray(v[r])) for r in range(N)]
    return np.stack([a for a, b in q]), np.stack([mx_ref.plane(b, rng) for a, b in q])
def values_of_codes():
    e, c = np.zeros((128, 128, 4), np.float32), np.zeros((128, 2, 4), np.uint8)
    e[np.arange(128), np.arange(128), 0] = 1
    c[:127, :, 0] = np.arange(256).reshape(2, 128).T[:127]
    return mx_ref.matmul(mx_ref.quantize(e.reshape(128, 512).astype(BF)), (c.reshape(128, 8), np.full((16, 2), 127, np.uint8))).T.reshape(-1).astype(np.float64)
CODE_VALUE, SCALE_VALUE = values_of_codes(), 2.0 ** (np.arange(256) - 127.0)
def decode(q):
    return (CODE_VALUE[q[0]].reshape(16, 8, -1, 4) * SCALE_VALUE[q[1]][:, None, :, None] + 0.0).reshape(128, -1).astype(np.float32)
def f(rng, *shape):
    return mx_ref.flush((rng.standard_normal(shape, dtype=np.float32) * np.exp2(rng.integers(-2, 3, shape[:-1] + (1,)))).astype(BF))
def wide(rng, *shape, cols=0):
    v = rng.standard_normal(shape, dtype=np.float32) * np.exp2(rng.integers(-12, 13, shape)).astype(np.float32)
    if cols: v *= np.repeat(np.exp2(rng.integers(-cols, cols + 1, shape[:-2] + (1, shape[-1] // 4))) * (rng.random(shape[:-2] + (1, shape[-1] // 4)) > 0.0625), 4, axis=-1).astype(np.float32)
    return mx_ref.flush(v.astype(BF))
C, R = 448, 2
SETS = np.arange(256)
ONE = (1 << np.arange(8))[:, None]
DECIDE = [16 * g + k for g in range(8) for k in range(10)] + [15]
def bits(b):
    return np.packbits(b, axis=-2, bitorder="little")[..., 0, :].astype(np.int64)
def numbers_of(rng):
    return {"x": np.array(f(rng, N, 128, 4 * C)), "u": np.array(f(rng, N, 128, 512)), "v": np.array(f(rng, N, 128, 512))}
def same(rng, w):
    c, s = packed(np.stack([w] * N), rng)
    return {"wc": c, "ws": np.stack([s[0]] * N)}
def weights(rng, keep=np.ones((8, 16), bool)):
    w = f(rng, 128, 2048).astype(np.float32).reshape(8, 16, 4, 8, 16, 4)
    w = np.where(keep[:, :, None, None, None, None] & keep[:, :, None], w, np.float32(0.0))
    return same(rng, w.reshape(128, 2048).astype(BF))
def setup_inputs(rng):
    return {**numbers_of(rng), **weights(rng)}
def setup_inputs_ties(rng):
    d = numbers_of(rng)
    e = rng.permutation(N)
    x = d["x"].reshape(N, 8, 16, C, 4)
    x[:, :, 0] = rng.integers(0, 3, (N, 8, C, 4)).astype(np.float32).astype(BF)
    x[e[0], 0, 0, :, 3] = 2.0
    x[e[1]] = 0.0
    u = d["u"].reshape(N, 128, 128, 4)
    u[:, :, DECIDE] = 0.0
    for g in range(8):
        u[:, 16 * g, 16 * g, 0] = 1.0
        u[:, 16 * g, 16 * g + 1, 1] = 1.0
        for k in range(8): u[:, 16 * ((g + k) % 8), 16 * g + 2 + k, 2] = 1.0
    u[:, 0, 15, 3] = 1.0
    u[e[2], 0, 15, 3] = -1.0
    keep = np.ones((8, 16), bool)
    keep[:, 0] = False
    return {"x": x.reshape(N, 128, 4 * C), "u": u.reshape(N, 128, 512), "v": d["v"], **weights(rng, keep)}
def setup_inputs_near(rng):
    d = numbers_of(rng)
    x = d["x"].astype(np.float32).reshape(N, 8, 16, C, 4)
    digits = lambda a: ((a[..., None] >> np.arange(4)) & 1) * np.exp2(np.arange(4) - 23.0)
    o = rng.permutation(N)
    n = rng.integers(0, 16, (N, 8, 3, C))
    far = []
    for r in range(N):
        if o[r] % 2 == 0:
            j, g = int(rng.integers(C)), int(rng.integers(5))
            n[r, :, 0, j] = 0
            n[r, g, 0, j] = 15
            n[r, g, 1, j] = 0
            far.append((r, j))
    have = n[:, :, 0] > n[:, :, 1]
    kind = np.where(have[:, 7], np.where(have[:, 6], 2, 1), 0)
    s = digits(2 * (7 - np.count_nonzero(have[:, :7], axis=1)) + rng.integers(0, 2, (N, C)))
    x[:, :, 8:] = 0
    x[:, 5:, :8] = 0
    x[:, :, 8:11] = digits(n)
    x[:, :, 11, :, 0] = 2.0 ** -10
    x[:, 7, 0, :, 0] = 1.0
    for k in range(2):
        x[:, k, 12] = s * (kind == k)[:, :, None]
        x[:, k, 13, :, 0] = (kind == k) * 2.0 ** -10
        x[:, 7 - k, 1, :, 0] = kind == k
    x[:, 5, 1, :, 0] = np.where(kind == 2, -(1.0 + 0.125 * rng.integers(0, 3, (N, C))) * 2.0 ** -30, 0.0)
    for r, j in far: x[r, 7, 1, j, 0] = 2.0 ** 30
    u = d["u"].reshape(N, 128, 128, 4)
    u[:, :, DECIDE] = 0.0
    for r in range(N):
        k = 2.0 ** -30 if o[r] < N // 2 else 1.0
        for g in range(8):
            for i in range(10):
                h = 16 * g + i
                u[r, 112, h, 0] = k
                u[r, 16 * g + 11, h, 0] = k
                u[r, 16 * g + 8 + i if i < 2 else 16 * ((g + i - 2) % 8) + 10, h] = k
    for p, k in ((113, 1.0), (13, 1.0), (97, 2.0 ** -30), (29, 2.0 ** -30), (81, 2.0 ** -30)): u[:, p, 15, 0] = k
    u[:, 12, 15] = 1.0
    u[:, 28, 15] = 2.0 ** -30
    keep = np.zeros((8, 16), bool)
    keep[:5, :8] = True
    return {"x": x.reshape(N, 128, 4 * C).astype(BF), "u": u.reshape(N, 128, 512), "v": d["v"], **weights(rng, keep)}
def setup_inputs_huge(rng):
    d = numbers_of(rng)
    c = rng.integers(0, 2, (N, 1, 1, C, 1)) * 2.0 - 1.0
    x = (0.9 + 0.05 * rng.random((N, 8, 16, C, 4))) * 2.0 ** 30 * c
    u = d["u"].reshape(N, 128, 128, 4)
    u[:, :, DECIDE] = 0.0
    for r in range(N):
        for h in DECIDE[:-1]: u[r, rng.permutation(128)[:64], h] = 2.0 ** 30
        u[r, :, 112] = 0.0
        u[r, :, 15] = (2.0 ** 30 * (1.0 - 0.03 * rng.random((128, 4)))).astype(np.float32).astype(BF)
    w = np.zeros((128, 4, 128, 4), np.float32)
    i = np.arange(128)
    for b in range(4): w[i, b, i, b] = -0.5
    return {"x": x.astype(np.float32).reshape(N, 128, 4 * C).astype(BF), "u": u.reshape(N, 128, 512), "v": d["v"], **same(rng, w.reshape(128, 2048).astype(BF))}
def setup_inputs_few(rng):
    d = numbers_of(rng)
    e = rng.permutation(N)
    x = d["x"].reshape(N, 8, 16, C, 4)
    k = (1.0 + (2 * rng.integers(0, 64, (N, 8, 8, C, 4)) + 1) * 2.0 ** -7) * np.exp2(-rng.integers(8, 15, (N, 8, 8, C, 4)).astype(np.float32))
    x[:, :, 8:] = (k * rng.choice([-1.0, 1.0], (N, 8, 8, C, 4))).astype(np.float32).astype(BF)
    x[:, :, 8, :, 0] = 1.96875
    have = rng.random((N, 8, C)) < 0.5
    have[e[0]] = True
    have[e[1]] = False
    have[e[2]] = np.arange(8)[:, None] == rng.integers(0, 7, C)
    j = int(rng.integers(C))
    have[e[3], 0, j] = False
    have[e[3], 1:, j] = True
    have[:, 7] = False
    x[:, :, 0, :, 0] = np.where(have, 1.0, -1.0).astype(np.float32).astype(BF)
    x[e[3], 0, 2, :, 0] = np.where(have[e[3], 0], -1.0, 1.0).astype(np.float32).astype(BF)
    s = rng.integers(-8, 9, (N, C))
    s[e[0]] = 64 + 8 * rng.integers(0, 8, C)
    s[e[0], C - 1] = 128
    x[:, 0, 1, :, 0] = s.astype(np.float32).astype(BF)
    u = d["u"].reshape(N, 128, 128, 4)
    u[:, :, ::16] = 0.0
    u[:, :, 1::16] = 0.0
    u[:, :, 15] = 0.0
    for h in range(0, 128, 16): u[:, h, h, 0] = 1.0
    u[:, 1, 15, 0] = 1.0
    u[e[3], 112, 112, 0] = 0.0
    u[e[3], 2, 112, 0] = 1.0
    u[e[3], :, 9] = 0.0
    w = f(rng, 128, 2048).astype(np.float32).reshape(8, 16, 4, 8, 16, 4)
    w[:, :, :, :, 8:] = 0
    i = np.arange(8)
    for p in range(8, 16):
        for b in range(4): w[i, p, b, i, p, b] = 32.0
    w[:, 8, 0, :, 8, 0] = 0
    w[:, :, 0, 0, 2] = 0
    w[0, 0, 0, 0, 2, 0] = -64.0
    w[:, :, 0, 7, 0] = 0
    return {"x": x.reshape(N, 128, 4 * C), "u": u.reshape(N, 128, 512), "v": d["v"], **same(rng, w.reshape(128, 2048).astype(BF))}
def setup_inputs_spread(rng):
    d = setup_inputs(rng)
    d["x"] = wide(rng, N, 128, 4 * C, cols=6)
    return d
def check_inputs(d):
    b = []
    for k in ("x", "u", "v"):
        a = np.abs(d[k].astype(np.float32))
        if not (np.isfinite(a).all() and ((a == 0) | (a >= 2.0 ** -30) & (a <= 2.0 ** 30)).all()): b.append("a value of " + k)
    if ((d["wc"] & 0x7F) == 0x7F).any(): b.append("a code of wc that is no number")
    for k in ("wc", "ws"):
        if (d[k] != d[k][:1]).any(): b.append(k + " isn't the same on all ranks")
    none, least, most = [emit(mx_ref.quantize(np.full((128, 16), k, np.float32).astype(BF)))[1][0, 0] for k in (0.0, 2.0 ** -30, 2.0 ** 30)]
    for r in range(N):
        a = mx_ref.live(d["ws"][r])
        if not ((a == none) | (a >= least) & (a <= most)).all(): b.append("a scale of ws")
    return b
def reference(x, u, v, wc, ws):
    qu = [mx_ref.quantize(u[r]) for r in range(N)]
    lay = pk(wc[0], ws[0])
    now = [x[r] for r in range(N)]
    for t in range(R):
        q = [mx_ref.quantize(now[r]) for r in range(N)]
        best, rep = np.zeros((N, 256), np.float32), np.zeros((N, 256), np.int64)
        here, want = np.zeros((N, 8, C), bool), np.zeros((N, 8, C), np.int64)
        for r in range(N):
            s = mx_ref.matmul(qu[r], q[r]) + np.float32(0.0)
            a = s.reshape(8, 16, C)
            here[r] = a[:, 0] > a[:, 1]
            m = bits(here[r])
            want[r] = (m & bits(a[:, 2:10] > a[:, 1:2])) | ONE
            holds = (m & SETS[:, None]) == SETS[:, None]
            strong = np.where(holds, s[15], np.float32(-np.inf))
            rep[r] = np.argmax(strong, axis=1)
            best[r] = np.max(strong, axis=1)
        win = np.argmax(best, axis=0)
        got = pick(join(*q), np.where(np.isfinite(best[win, SETS]), C * win + rep[win, SETS], -1))
        made = tile([mx_ref.matmul(pick(lay, np.arange(128 * b, 128 * b + 128)), got) * np.float32(0.03125) for b in range(4)])
        table = decode(mx_ref.quantize(made)).astype(BF)
        for r in range(N):
            now[r] = (now[r].astype(np.float32) + gcols(table, np.where(here[r], -1, want[r])).astype(np.float32)).astype(BF)
    y, wl = np.zeros((N, 128, C), np.float32), np.zeros((N, 8, C), np.float32)
    oc, osc = np.zeros((N, 128, 4 * C), np.uint8), np.zeros((N, 16, C), np.uint8)
    for r in range(N):
        q = mx_ref.quantize(now[r])
        y[r] = mx_ref.matmul(mx_ref.quantize(v[r]), q)
        wl[r] = want[r]
        oc[r], osc[r] = emit(q)
    return {"y": y, "wl": wl, "oc": oc, "osc": osc}

@@ -1,0 +1,457 @@
+from concourse.bass import DstId, RemoteDMATransfer
+from concourse.mybir import dt, AluOpType, AxisListType, ActivationFunctionType
+
+F8, U8, U16, I32, F32, BF = "float8_e4m3fn_x4", "uint8", "uint16", "int32", "float32", "bfloat16"
+ROUNDS, COLS, BIG = 2, 448, 2.0 ** 30
+CUT = 224
+SCRATCH = {}
+
+
+def buf(name, n, dtype, where="sbuf"):
+    SCRATCH[name] = (where, [128, n], dtype)
+
+
+for _k in range(3):
+    buf("xt%d" % _k, 1800, BF)
+    buf("x%d_q" % _k, 450, F8)
+    buf("x%d_s" % _k, 450, U8)
+for _k in range(2):
+    for _n, _w in (("c", 192), ("l", 256), ("t", 128), ("h", 128), ("z", 192)):
+        buf("%s%d_q" % (_n, _k), _w, F8)
+        buf("%s%d_s" % (_n, _k), _w, U8)
+    buf("wst%d" % _k, 16, F32)
+    buf("lst%d" % _k, 16, F32)
+    buf("mk%d" % _k, 456, F32)
+    buf("ru%d" % _k, 456, F32)
+    buf("jk%d" % _k, 448, BF)
+for _n, _w in (("u", 128), ("v", 128), ("up", 256), ("w", 512), ("f", CUT), ("i", 128), ("a", 128),
+               ("kh", 512), ("kx", 128), ("kb", 256), ("ko", 128), ("ke", 512), ("kw", 512)):
+    buf(_n + "_q", _w, F8)
+    buf(_n + "_s", _w, U8)
+for _n, _w in (("ut", 512), ("vt", 512), ("dd", 448), ("ft", 4 * CUT), ("id", 128), ("vv", 512), ("hh", 512), ("yy", 1040),
+               ("ww", 448), ("an", 512), ("kh", 2048), ("kx", 512), ("kb", 1024), ("ko", 512), ("ke", 2048),
+               ("jb", 128), ("jq", 128), ("r16", 256), ("bt", 128)):
+    buf(_n, _w, BF)
+for _n, _w in (("bc", 448), ("sb", 456), ("ix", 2), ("xb", 16), ("gm", 256), ("gs", 256), ("sel", 8), ("mx8", 8), ("gg", 8),
+               ("f4", 4), ("e4", 4), ("o4", 4), ("yo", 448), ("wlb", 448), ("cf", 32), ("lm", 256), ("kp", 256), ("b8", 8),
+               ("ib8", 8), ("mk8", 8), ("tab", 112)):
+    buf(_n, _w, F32)
+for _n, _w in (("ci", 8), ("ij", 128), ("ijt", 128), ("iju", 128), ("iu", 8)):
+    buf(_n, _w, I32)
+for _n, _w in (("ou", 16), ("oz", 4), ("of1", 16), ("oft", 4), ("ofx", 112)):
+    buf(_n, _w, U16)
+PSUM = ["b%d" % _k for _k in range(8)]
+for _n in PSUM:
+    buf(_n, 512, F32, "psum")
+SEMAPHORES = (["v", "a", "t", "gp", "sent", "stored", "dx0", "dx1", "du", "dv", "dwc", "dws"]
+              + ["%s%d" % (n, k) for n in ("lc", "lp", "lt", "hc", "hp") for k in range(2)])
+
+
+def rank_program(g, core, T, topo):
+    r = T.rank_of(core)
+    if r is None:
+        return
+    A, ACT = AluOpType, ActivationFunctionType
+    queues = {"v": g.vector, "a": g.scalar, "t": g.tensor, "g": g, "s": g.sync}
+    own_sem = {"v": "v", "a": "a", "t": "t", "g": "gp"}
+    total, know, snap, acc = {}, {q: {} for q in queues}, {}, {}
+
+    def R(name, lo=0, hi=None, step=1):
+        return (name, lo, SCRATCH[name][1][1] if hi is None else hi, step)
+
+    def V(x):
+        return T[x[0]][:, x[1]:x[2]] if x[3] == 1 else T[x[0]][:, x[1]:x[2]:x[3]]
+
+    def hit(p, q):
+        if max(p[1], q[1]) >= min(p[2], q[2]):
+            return False
+        return p[3] != q[3] or (p[1] - q[1]) % p[3] == 0
+
+    def wait(q, tok):
+        sem, val = tok
+        if know[q].get(sem, 0) >= val:
+            return
+        queues[q].wait_ge(T.sem[sem], val)
+        for s, x in list(snap.get(tok, {}).items()) + [tok]:
+            know[q][s] = max(know[q].get(s, 0), x)
+
+    def deps(q, lane, reads, writes):
+        need = set()
+        for reg, isw in [(x, False) for x in reads] + [(x, True) for x in writes]:
+            for old, oldw, oldlane, tok in acc.get(reg[0], []):
+                if reg[0] in PSUM:
+                    if oldlane == lane:
+                        continue
+                elif not (isw or oldw) or not hit(old, reg):
+                    continue
+                need.add(tok)
+        for tok in sorted(need, key=lambda x: -x[1]):
+            wait(q, tok)
+
+    def note(lane, tok, reads, writes):
+        for reg, isw in [(x, False) for x in reads] + [(x, True) for x in writes]:
+            acc.setdefault(reg[0], []).append((reg, isw, lane, tok))
+
+    def op(q, fn, writes, reads):
+        deps(q, q, reads, writes)
+        s = own_sem[q]
+        total[s] = total.get(s, 0) + 1
+        tok = (s, total[s])
+        fn().then_inc(T.sem[s], 1)
+        snap[tok] = dict(know[q])
+        note(q, tok, reads, writes)
+
+    def dma(q, sem, out, in_, writes, reads):
+        deps(q, "dma", reads, writes)
+        total[sem] = total.get(sem, 0) + 16
+        queues[q].dma_start(out, in_).then_inc(T.sem[sem], 16)
+        tok = (sem, total[sem])
+        snap[tok] = dict(know[q])
+        note("dma", tok, reads, writes)
+
+    def memset(o, c):
+        op("v", lambda: g.vector.memset(V(o), c), [o], [])
+
+    def copy(o, i):
+        op("v", lambda: g.vector.tensor_copy(V(o), V(i)), [o], [i])
+
+    def tt(o, i, j, f):
+        op("v", lambda: g.vector.tensor_tensor(V(o), V(i), V(j), f), [o], [i, j])
+
+    def ts(o, i, s1, f1, s2=None, f2=None):
+        v = lambda s: V(s) if isinstance(s, tuple) else s
+        rd = [i] + [s for s in (s1, s2) if isinstance(s, tuple)]
+        if f2 is None:
+            op("v", lambda: g.vector.tensor_scalar(V(o), V(i), v(s1), None, f1), [o], rd)
+        else:
+            op("v", lambda: g.vector.tensor_scalar(V(o), V(i), v(s1), v(s2), f1, f2), [o], rd)
+
+    def red(o, i):
+        op("v", lambda: g.vector.tensor_reduce(V(o), V(i), AxisListType.X, A.add), [o], [i])
+
+    def scan(o, i, j, init, f1, f2):
+        op("v", lambda: g.vector.tensor_tensor_scan(V(o), V(i), V(j), init, f1, f2), [o], [i, j])
+
+    def act(o, i, scale=1.0):
+        op("a", lambda: g.scalar.activation(V(o), V(i), ACT.Copy, scale=scale), [o], [i])
+
+    def iota(o, pattern, base, ch):
+        if SCRATCH[o[0]][2] == I32:
+            op("g", lambda: g.iota(V(o), pattern, base, ch), [o], [])
+        else:
+            op("g", lambda: g.iota(V(o), pattern, base, ch, allow_small_or_imprecise_dtypes=True), [o], [])
+
+    def quant(m, lo, hi, i):
+        q, s = R(m + "_q", lo, hi), R(m + "_s", lo, hi)
+        op("v", lambda: g.vector.quantize_mx(V(q), V(s), V(i)), [q, s], [i])
+
+    def mm(bank, w, wlo, m, mlo, n):
+        o = R(bank, 0, n)
+        i = [R(w + "_q", wlo, wlo + 128), R(w + "_s", wlo, wlo + 128), R(m + "_q", mlo, mlo + n), R(m + "_s", mlo, mlo + n)]
+        op("t", lambda: g.tensor.matmul_mx(V(o), V(i[0]), V(i[1]), V(i[2]), V(i[3]), True, True), [o], i)
+
+    def pick(o, lo, hi, w, wide, f):
+        q, s, wq, wp = R(o + "_q", lo, hi), R(o + "_s", lo, hi), R(w + "_q", 0, wide), R(w + "_s", 0, wide)
+        op("v", lambda: g.vector.tensor_copy(V(q).bitcast(dt.uint32), V(wq).bitcast(dt.uint32).indirect(V(f))), [q], [wq, f])
+        op("a", lambda: g.scalar.activation(V(s), V(wp).indirect(V(f)), ACT.Copy), [s], [wp, f])
+
+    def cf(k):
+        return R("cf", k, k + 1)
+
+    def tab(k, n=8):
+        return R("tab", k, k + n)
+
+    others = [r ^ d for d in (1, 2, 3)]
+    eng = topo.engines(core, T.cores[others[0]])
+    bits = lambda es: sum(1 << e for e in es)
+    half, quarter = len(eng) // 2, len(eng) // 4
+    one, two = eng[:half], eng[half:]
+    cut = lambda es: [es[:quarter], es[quarter:]]
+    split = [[one] + cut(two), [cut(one)[0], two, cut(one)[1]], cut(two) + [one]]
+
+    def dest(o):
+        rid, pid, _ = topo.addr(T.cores[o])
+        return DstId(rid=rid, pnc=pid)
+
+    def view(x, codes):
+        return V(x).bitcast(dt.uint8) if codes else V(x)
+
+    def scatter(kind, src, dst, sem):
+        deps("g", "rem", [src(o) for o in others], [])
+        g.remote_dma_fused([RemoteDMATransfer(dst_ids=[dest(o)], dma_engine_mask=bits(split[kind][d]), remote_sem=T.sem[sem],
+                                              src=view(src(o), kind == 0), dst=view(dst(o), kind == 0))
+                            for d, o in enumerate(others)], local_sem=T.sem.sent)
+        total["sent"] = total.get("sent", 0) + len(eng)
+
+    def spread(codes, src, dst, sem):
+        deps("g", "rem", [src], [])
+        g.remote_dma_fused([RemoteDMATransfer(dst_ids=[dest(o) for o in others], dma_engine_mask=bits(eng), remote_sem=T.sem[sem],
+                                              srcs=[view(src, codes)], dsts=[view(dst(o), codes) for o in others])],
+                           local_sem=T.sem.sent)
+        total["sent"] = total.get("sent", 0) + len(eng)
+
+    STRONG = [0, 8, 4, 12]
+    for k in range(ROUNDS):
+        for sem, val, regs in (("lc%d", len(eng), [R("l%d_q" % k, 64 * o, 64 * o + 64) for o in others]),
+                               ("lp%d", len(eng), [R("l%d_s" % k, 64 * o, 64 * o + 64) for o in others]),
+                               ("lt%d", len(eng), [R("lst%d" % k, STRONG[o], STRONG[o] + 4) for o in others]),
+                               ("hc%d", 3 * len(eng), [R("z%d_q" % k)]),
+                               ("hp%d", 3 * len(eng), [R("z%d_s" % k)])):
+            total[sem % k] = val
+            note("rem", (sem % k, val), [], regs)
+
+    dma("s", "dx0", T.xt0[:, 0:4 * CUT], T.x[:, 0:4 * CUT], [R("xt0", 0, 4 * CUT)], [])
+    dma("a", "du", V(R("ut")), T.u[:, :], [R("ut")], [])
+    dma("s", "dx1", T.xt0[:, 4 * CUT:1792], T.x[:, 4 * CUT:1792], [R("xt0", 4 * CUT, 1792)], [])
+    wait("s", ("dx1", 16))
+    dma("s", "dwc", V(R("w_q")).bitcast(dt.uint8), T.wc[:, :], [R("w_q")], [])
+    dma("s", "dws", V(R("w_s")), T.ws[:, :], [R("w_s")], [])
+    dma("s", "dv", V(R("vt")), T.v[:, :], [R("vt")], [])
+
+    iota(R("ci", 0, 1), [[0, 1]], 0, 1)
+    iota(R("iu"), [[16, 8]], 1, 0)
+    iota(R("jb"), [[1, 128]], 0, 0)
+    iota(R("ij"), [[-64, 2], [1, 64]] if r & 1 else [[64, 2], [1, 64]], 64 * (r & 1), 0)
+    iota(R("r16"), [[0, 16], [1, 16]], 0, 0)
+    iota(R("ib8"), [[128, 2], [16, 4]], 0, 0)
+    iota(R("jq"), [[1, 32], [0, 4]], 0, 0)
+    P, LANE, GRP, B4, IPW, HSC, C112, PWS, S1, S2, WG0, WG1, PLB, NZ, CAB, LM2 = [cf(k) for k in range(15)] + [cf(20)]
+
+    memset(R("xt0", 1792, 1800), 0.0)
+    memset(R("ft"), 0.0)
+    memset(R("kh"), 0.0)
+    memset(R("ou", 8, 16), 15)
+    copy(R("ou", 0, 8), R("iu"))
+    ts(R("ci", 1, 2), R("ci", 0, 1), 15, A.bitwise_and)
+    ts(R("ci", 2, 3), R("ci", 0, 1), 4, A.arith_shift_right)
+    copy(P, R("ci", 0, 1))
+    memset(tab(80), 0.5)
+    memset(tab(16, 16), 0.0)
+    copy(LANE, R("ci", 1, 2))
+    copy(GRP, R("ci", 2, 3))
+    scan(tab(96), tab(80), tab(16), 256.0, A.mult, A.add)
+    ts(R("mk8"), R("jb", 0, 8), GRP, A.is_equal)
+    ts(HSC, LANE, 0.0, A.is_equal, -2.0 ** 23, A.mult)
+    ts(C112, P, 112.0, A.is_equal, -BIG, A.mult)
+    tt(tab(80), R("mk8"), tab(96), A.mult)
+    red(IPW, tab(80))
+    ts(R("ijt"), R("ij"), IPW, A.mult)
+    ts(R("iju"), R("ijt"), 128, A.bitwise_and)
+    ts(R("bt"), R("iju"), HSC, A.mult)
+    for h in range(2):
+        for e in range(2):
+            o = R("kh", 1024 * h + 513 * e, 1024 * h + 512 * e + 512, 4)
+            if h ^ r >> 1:
+                ts(o, R("bt"), C112, A.min)
+            else:
+                act(o, R("bt"))
+    quant("u", 0, 128, R("ut"))
+    pick("up", 0, 256, "u", 128, R("ou"))
+
+    def const_index():
+        for e in range(4):
+            ts(R("kx", e, 512, 4), R("r16", 0, 128), LANE, A.is_equal)
+        memset(R("vv"), 0.0)
+        quant("kx", 0, 128, R("kx"))
+        for k in range(2):
+            memset(R("mk%d" % k, 448, 456), -2.0 ** 59)
+        memset(R("sb", 448, 456), -2.0 ** 59)
+
+    def const_strength():
+        ts(R("lm"), R("r16"), LANE, A.is_equal)
+        ts(R("kp"), R("r16"), 0.0, A.not_equal)
+        ts(R("b8"), R("ib8"), LANE, A.add, 0.015625, A.mult)
+
+    def const_flags():
+        memset(R("oz"), COLS)
+        memset(R("an", 448, 512), 0.0)
+        ts(CAB, LANE, 0.0, A.not_equal, 100.0, A.mult)
+        tt(CAB, CAB, GRP, A.add)
+        ts(CAB, CAB, 2.0, A.add)
+        for e in range(2):
+            ts(R("kb", 512 * e + e, 512 * e + 512, 4), R("r16", 0, 128), CAB, A.is_equal)
+        quant("kb", 0, 256, R("kb"))
+
+    def diagonal():
+        for b in range(4):
+            act(R("ke", 512 * b + b, 512 * b + 512, 4), R("id"))
+
+    def const_lists():
+        memset(tab(0, 16), 2.0)
+        ts(R("ci", 3, 4), R("ci", 1, 2), 3, A.bitwise_and)
+        ts(LM2, LANE, 2.0, A.subtract)
+        scan(tab(32, 16), tab(0, 16), tab(16, 16), 0.5, A.mult, A.add)
+        copy(B4, R("ci", 3, 4))
+        tt(NZ, LM2, GRP, A.not_equal)
+        ts(tab(80, 16), R("r16", 0, 16), LANE, A.is_equal)
+        copy(tab(48, 16), tab(32, 16))
+        copy(tab(104), tab(32))
+        memset(tab(48, 2), 0.0)
+        memset(tab(58, 6), 0.0)
+        copy(tab(64, 16), tab(48, 16))
+        for k in range(2):
+            if r >> k & 1:
+                ts(tab(72 + k, 1), tab(56 + k, 1), -1.0, A.mult)
+                ts(tab(110 + k, 1), tab(38 + k, 1), -1.0, A.mult)
+        memset(tab(64, 1), 2048.0)
+        tt(tab(96), R("mk8"), tab(104), A.mult)
+        tt(tab(0, 16), tab(80, 16), tab(64, 16), A.mult)
+        red(PWS, tab(96))
+        red(WG0, tab(0, 16))
+        ts(S1, PWS, 4.0, A.mult, 256.0 * r, A.add)
+        tt(WG0, WG0, NZ, A.mult)
+        tt(S1, S1, B4, A.add)
+        ts(S2, B4, 1024.0, A.add)
+        for e in range(4):
+            ts(cf(16 + e), GRP, 4.0, A.mult, float(e), A.add)
+        for e in range(4):
+            ts(R("ko", e, 512, 4), R("jq"), cf(16 + e), A.is_equal, WG0, A.mult)
+        quant("ko", 0, 128, R("ko"))
+
+    def const_wl():
+        tt(tab(0, 16), tab(80, 16), tab(48, 16), A.mult)
+        red(WG1, tab(0, 16))
+        ts(tab(96), R("jb", 0, 8), P, A.is_equal)
+        ts(WG1, WG1, NZ, A.mult, 0.25, A.mult)
+        tt(tab(96), tab(96), tab(32), A.mult)
+        ts(R("id"), R("jb"), GRP, A.is_equal, WG1, A.mult)
+        red(PLB, tab(96))
+        diagonal()
+        quant("kw", 0, 512, R("ke"))
+
+    chunks = ((0, CUT), (CUT, COLS))
+
+    def quant_state(k, c):
+        lo, hi = chunks[c][0], chunks[c][1] + 2 * c
+        quant("x%d" % k, lo, hi, R("xt%d" % k, 4 * lo, 4 * hi))
+
+    for c in range(2):
+        quant_state(0, c)
+    quant("kh", 0, 512, R("kh"))
+
+    for k in range(ROUNDS):
+        X, state = "x%d" % k, "xt%d" % k
+        C, L, TT, H, Z = ["%s%d" % (n, k) for n in "clthz"]
+        last = k == ROUNDS - 1
+        for c, (lo, hi) in enumerate(chunks):
+            mm("b%d" % (2 * c), "up", 0, X, lo, hi - lo)
+            mm("b%d" % (2 * c + 1), "u", 0, X, lo, hi - lo)
+            act(R("bc", lo, hi), R("b%d" % (2 * c), 0, hi - lo))
+        mm("b4", "up", 128, X, 0, COLS)
+        act(R("sb", 0, COLS), R("b4", 0, COLS), 2.0 ** -12)
+        for c, (lo, hi) in enumerate(chunks):
+            tt(R("dd", lo, hi), R("b%d" % (2 * c + 1), 0, hi - lo), R("bc", lo, hi), A.subtract)
+            ts(R("ft", c, c + 4 * (hi - lo) - 3, 4), R("dd", lo, hi), 0.0, A.is_le, BIG, A.mult)
+        quant("f", 0, CUT, R("ft"))
+        banks = [["b5", "b6"], ["b7", "b0"]]
+        for h in range(2):
+            for c, (lo, hi) in enumerate(chunks):
+                mm(banks[h][c], "kh", 128 * (2 * h + c), "f", 0, hi - lo)
+        if k == 0:
+            const_index()
+        for h in range(2):
+            m, u = "mk%d" % h, "ru%d" % h
+            for c, (lo, hi) in enumerate(chunks):
+                tt(R(m, lo, hi), R(banks[h][c], 0, hi - lo), R("sb", lo, hi), A.add)
+            scan(R(u, 0, 449), R(m, 0, 449), R(m, 0, 449), -2.0 ** 62, A.max, A.max)
+            i = R("ix", h, h + 1)
+            op("a", lambda: g.scalar.activation(V(R("jk%d" % h)), V(R(u, 0, COLS)), ACT.Sign, bias=V(R(u, COLS, COLS + 1)),
+                                                scale=-1.0, accum_out=V(i)), [R("jk%d" % h), i], [R(u, 0, 449)])
+        if k == 0:
+            const_strength()
+        for h in range(2):
+            ts(R("xb", 8 * h, 8 * h + 8), R("mk8"), R("ix", h, h + 1), A.mult)
+        ts(R("vv", 0, 64, 4), R("xb"), 402653184.0, A.add, -402653184.0, A.add)
+        tt(R("vv", 1, 64, 4), R("xb"), R("vv", 0, 64, 4), A.subtract)
+        quant("i", 0, 128, R("vv"))
+        mm("b1", "kx", 0, "i", 0, 128)
+        copy(R("of1"), R("b1", 0, 16))
+        place = lambda o, n: n * (r ^ o)
+        W, S = "wst%d" % k, "lst%d" % k
+        pick(C, 0, 192, X, 450, R("of1", 4, 16))
+        scatter(0, lambda o: R(C + "_q", place(o, 64) - 64, place(o, 64)), lambda o: R(L + "_q", 64 * r, 64 * r + 64), "lc%d" % k)
+        op("v", lambda: g.vector.tensor_tensor(V(R("gm")), V(R("sb", 0, 450)).indirect(V(R("of1"))), V(R("lm")), A.mult),
+           [R("gm")], [R("sb", 0, 450), R("of1"), R("lm")])
+        scan(R("gs"), R("kp"), R("gm"), 0.0, A.mult, A.add)
+        copy(R(W), R("gs", 15, 256, 16))
+        scatter(1, lambda o: R(W, place(o, 4), place(o, 4) + 4), lambda o: R(S, STRONG[r], STRONG[r] + 4), "lt%d" % k)
+        scatter(2, lambda o: R(C + "_s", place(o, 64) - 64, place(o, 64)), lambda o: R(L + "_s", 64 * r, 64 * r + 64), "lp%d" % k)
+        if k == 0:
+            act(R("kb"), R("kh", 0, 1024), 0.0)
+        pick(L, 64 * r, 64 * r + 64, X, 450, R("of1", 0, 4))
+        copy(R(S, STRONG[r], STRONG[r] + 4), R(W, 0, 4))
+        if k == 0:
+            const_flags()
+        pick(TT, 64, 128, X, 450, R("oz"))
+        ts(R("ww"), R("dd"), 0.0, A.is_gt)
+        for c, (lo, hi) in enumerate(chunks):
+            mm("b%d" % (2 + c), "kb", 128 * c, "f", 0, hi - lo)
+            tt(R("an", lo, hi), R("ww", lo, hi), R("b%d" % (2 + c), 0, hi - lo), A.is_gt)
+        quant("a", 0, 128, R("an"))
+        if k == 0:
+            ts(R("id"), R("jb"), P, A.is_equal)
+            memset(R("hh"), 0.0)
+            memset(R("yy", 1024, 1040), 0.0)
+            act(R("ke"), R("kh"), 0.0)
+            diagonal()
+        if last:
+            const_wl()
+        tt(R("sel"), R(S, 8, 16), R(S, 0, 8), A.is_gt)
+        tt(R("mx8"), R(S, 8, 16), R(S, 0, 8), A.max)
+        tt(R("gg"), R("sel"), R("b8"), A.add)
+        tt(R("f4"), R("mx8", 4, 8), R("mx8", 0, 4), A.is_gt)
+        tt(R("e4"), R("f4"), R("gg", 4, 8), A.mult)
+        tt(R("o4"), R("e4"), R("gg", 0, 4), A.max)
+        ts(R("oft"), R("o4"), 64.0, A.mult)
+        pick(TT, 0, 64, L, 256, R("oft"))
+        hb = ["b5", "b6", "b7", "b0"]
+        for b in range(4):
+            mm(hb[b], "w", 128 * b, TT, 0, 128)
+            o, i = R("hh", b, 256, 4), R(hb[b], 0, 64)
+            if b % 2:
+                ts(o, i, 0.03125, A.mult)
+            else:
+                act(o, i, 0.03125)
+        quant(H, 0, 128, R("hh"))
+        slot = lambda o: 64 * ((r ^ o) - 1)
+        spread(True, R(H + "_q", 0, 64), lambda o: R(Z + "_q", slot(o), slot(o) + 64), "hc%d" % k)
+        spread(False, R(H + "_s", 0, 64), lambda o: R(Z + "_s", slot(o), slot(o) + 64), "hp%d" % k)
+        if k == 0:
+            quant("ke", 0, 512, R("ke"))
+            quant("v", 0, 128, R("vt"))
+        memset(R("xt%d" % (k + 1), 1792, 1800), 0.0)
+        ob = ["b1", "b2", "b3", "b4"]
+        for b in range(4):
+            mm(ob[b], "ke", 128 * b, H, 0, 128)
+            act(R("yy", b, 256, 4), R(ob[b], 0, 64))
+        if k == 0:
+            const_lists()
+        mm("b4", "ko", 0, "a", 0, 128)
+        ts(R("ofx"), R("b4", 0, 112), S1, A.add, S2, A.min)
+        if last:
+            for b in range(4):
+                mm(ob[b], "kw", 128 * b, "a", 0, 128)
+                o, i = R("wlb", b, COLS, 4), R(ob[b], 0, 112)
+                op("a", lambda: g.scalar.activation(V(o), V(i), ACT.Identity, bias=V(PLB)), [o], [i, PLB])
+            dma("s", "stored", T.wl[:, :], T.wlb[0:8, 0:COLS], [], [R("wlb")])
+        for b in range(4):
+            mm(hb[b], "ke", 128 * b, Z, 0, 192)
+            o, i = R("yy", 256 + b, 1024, 4), R(hb[b], 0, 192)
+            if b % 2:
+                copy(o, i)
+            else:
+                act(o, i)
+        for c, (lo, hi) in enumerate(chunks):
+            o, i, f = R("xt%d" % (k + 1), 4 * lo, 4 * hi), R(state, 4 * lo, 4 * hi), R("ofx", lo // 4, hi // 4)
+            op("v", lambda: g.vector.tensor_tensor(V(o), V(R("yy")).indirect(V(f)), V(i), A.add), [o], [R("yy"), f, i])
+            quant_state(k + 1, c)
+
+    for c, (lo, hi) in enumerate(chunks):
+        dma("s", "stored", T.oc[:, 4 * lo:4 * hi], V(R("x2_q", lo, hi)).bitcast(dt.uint8), [], [R("x2_q", lo, hi)])
+        mm("b%d" % c, "v", 0, "x2", lo, hi - lo)
+        act(R("yo", lo, hi), R("b%d" % c, 0, hi - lo))
+        dma("s", "stored", T.y[:, lo:hi], V(R("yo", lo, hi)), [], [R("yo", lo, hi)])
+    for q in range(4):
+        dma("a", "stored", T.osc[4 * q:4 * q + 4, :], T.x2_s[32 * q:32 * q + 4, 0:COLS], [], [R("x2_s", 0, COLS)])
+    for s in sorted(total):
+        wait("g", (s, total[s]))

@@ -2,8 +2,9 @@ from concourse.bass import DstId, RemoteDMATransfer
 from concourse.mybir import dt, AluOpType, AxisListType, ActivationFunctionType
 
 F8, U8, U16, I32, F32, BF = "float8_e4m3fn_x4", "uint8", "uint16", "int32", "float32", "bfloat16"
-ROUNDS, COLS, BIG = 2, 448, 2.0 ** 30
-CUT = 224
+ROUNDS, COLS = 2, 448
+CUT, TAIL = 256, 320
+SMALL, NONE, LEAST = 2.0 ** -42, -2.0 ** 29, -2.0 ** 34
 SCRATCH = {}
 
 
@@ -28,15 +29,15 @@ for _n, _w in (("u", 128), ("v", 128), ("up", 256), ("w", 512), ("f", CUT), ("i"
                ("kh", 512), ("kx", 128), ("kb", 256), ("ko", 128), ("ke", 512), ("kw", 512)):
     buf(_n + "_q", _w, F8)
     buf(_n + "_s", _w, U8)
-for _n, _w in (("ut", 512), ("vt", 512), ("dd", 448), ("ft", 4 * CUT), ("id", 128), ("vv", 512), ("hh", 512), ("yy", 1040),
+for _n, _w in (("ut", 512), ("vt", 512), ("ft", 4 * CUT), ("id", 128), ("km", 128), ("vv", 512), ("hh", 512), ("yy", 1040),
                ("ww", 448), ("an", 512), ("kh", 2048), ("kx", 512), ("kb", 1024), ("ko", 512), ("ke", 2048),
-               ("jb", 128), ("jq", 128), ("r16", 256), ("bt", 128)):
+               ("jb", 128), ("jq", 512), ("r16", 256), ("bt", 128)):
     buf(_n, _w, BF)
 for _n, _w in (("bc", 448), ("sb", 456), ("ix", 2), ("xb", 16), ("gm", 256), ("gs", 256), ("sel", 8), ("mx8", 8), ("gg", 8),
                ("f4", 4), ("e4", 4), ("o4", 4), ("yo", 448), ("wlb", 448), ("cf", 32), ("lm", 256), ("kp", 256), ("b8", 8),
                ("ib8", 8), ("mk8", 8), ("tab", 112)):
     buf(_n, _w, F32)
-for _n, _w in (("ci", 8), ("ij", 128), ("ijt", 128), ("iju", 128), ("iu", 8)):
+for _n, _w in (("ci", 8), ("ij", 128), ("ijt", 128), ("iju", 128), ("iu", 16)):
     buf(_n, _w, I32)
 for _n, _w in (("ou", 16), ("oz", 4), ("of1", 16), ("oft", 4), ("ofx", 112)):
     buf(_n, _w, U16)
@@ -132,8 +133,8 @@ def rank_program(g, core, T, topo):
     def scan(o, i, j, init, f1, f2):
         op("v", lambda: g.vector.tensor_tensor_scan(V(o), V(i), V(j), init, f1, f2), [o], [i, j])
 
-    def act(o, i, scale=1.0):
-        op("a", lambda: g.scalar.activation(V(o), V(i), ACT.Copy, scale=scale), [o], [i])
+    def act(o, i, scale=1.0, bias=0.0):
+        op("a", lambda: g.scalar.activation(V(o), V(i), ACT.Copy, bias=bias, scale=scale), [o], [i])
 
     def iota(o, pattern, base, ch):
         if SCRATCH[o[0]][2] == I32:
@@ -150,10 +151,17 @@ def rank_program(g, core, T, topo):
         i = [R(w + "_q", wlo, wlo + 128), R(w + "_s", wlo, wlo + 128), R(m + "_q", mlo, mlo + n), R(m + "_s", mlo, mlo + n)]
         op("t", lambda: g.tensor.matmul_mx(V(o), V(i[0]), V(i[1]), V(i[2]), V(i[3]), True, True), [o], i)
 
-    def pick(o, lo, hi, w, wide, f):
-        q, s, wq, wp = R(o + "_q", lo, hi), R(o + "_s", lo, hi), R(w + "_q", 0, wide), R(w + "_s", 0, wide)
+    def pick_codes(o, lo, hi, w, wide, f):
+        q, wq = R(o + "_q", lo, hi), R(w + "_q", 0, wide)
         op("v", lambda: g.vector.tensor_copy(V(q).bitcast(dt.uint32), V(wq).bitcast(dt.uint32).indirect(V(f))), [q], [wq, f])
+
+    def pick_scales(o, lo, hi, w, wide, f):
+        s, wp = R(o + "_s", lo, hi), R(w + "_s", 0, wide)
         op("a", lambda: g.scalar.activation(V(s), V(wp).indirect(V(f)), ACT.Copy), [s], [wp, f])
+
+    def pick(*a):
+        pick_codes(*a)
+        pick_scales(*a)
 
     def cf(k):
         return R("cf", k, k + 1)
@@ -167,7 +175,7 @@ def rank_program(g, core, T, topo):
     half, quarter = len(eng) // 2, len(eng) // 4
     one, two = eng[:half], eng[half:]
     cut = lambda es: [es[:quarter], es[quarter:]]
-    split = [[one] + cut(two), [cut(one)[0], two, cut(one)[1]], cut(two) + [one]]
+    split = [[one] + cut(two), [cut(one)[0], two, cut(one)[1]], cut(one) + [two]]
 
     def dest(o):
         rid, pid, _ = topo.addr(T.cores[o])
@@ -179,7 +187,7 @@ def rank_program(g, core, T, topo):
     def scatter(kind, src, dst, sem):
         deps("g", "rem", [src(o) for o in others], [])
         g.remote_dma_fused([RemoteDMATransfer(dst_ids=[dest(o)], dma_engine_mask=bits(split[kind][d]), remote_sem=T.sem[sem],
-                                              src=view(src(o), kind == 0), dst=view(dst(o), kind == 0))
+                                              src=view(src(o), kind == 0), dst=view(dst, kind == 0))
                             for d, o in enumerate(others)], local_sem=T.sem.sent)
         total["sent"] = total.get("sent", 0) + len(eng)
 
@@ -208,35 +216,43 @@ def rank_program(g, core, T, topo):
     dma("s", "dws", V(R("w_s")), T.ws[:, :], [R("w_s")], [])
     dma("s", "dv", V(R("vt")), T.v[:, :], [R("vt")], [])
 
+    P, LANE, GRP, B4, IPW, HSC, C112, PWS, S1, S2, WG0, WG1, PLB, NZ, CAB, LM2, GRP4 = [cf(k) for k in range(17)]
     iota(R("ci", 0, 1), [[0, 1]], 0, 1)
-    iota(R("iu"), [[16, 8]], 1, 0)
+    iota(P, [[0, 1]], 0, 1)
     iota(R("jb"), [[1, 128]], 0, 0)
+    iota(R("iu", 0, 8), [[16, 8]], 1, 0)
+    iota(R("iu", 8, 16), [[0, 8]], 15, 0)
     iota(R("ij"), [[-64, 2], [1, 64]] if r & 1 else [[64, 2], [1, 64]], 64 * (r & 1), 0)
+    iota(R("ft"), [[0, 4 * CUT]], 0, 0)
     iota(R("r16"), [[0, 16], [1, 16]], 0, 0)
     iota(R("ib8"), [[128, 2], [16, 4]], 0, 0)
-    iota(R("jq"), [[1, 32], [0, 4]], 0, 0)
-    P, LANE, GRP, B4, IPW, HSC, C112, PWS, S1, S2, WG0, WG1, PLB, NZ, CAB, LM2 = [cf(k) for k in range(15)] + [cf(20)]
+    iota(R("vv"), [[0, 512]], 0, 0)
+    iota(R("kb"), [[0, 1024]], 0, 0)
 
-    memset(R("xt0", 1792, 1800), 0.0)
-    memset(R("ft"), 0.0)
-    memset(R("kh"), 0.0)
-    memset(R("ou", 8, 16), 15)
-    copy(R("ou", 0, 8), R("iu"))
-    ts(R("ci", 1, 2), R("ci", 0, 1), 15, A.bitwise_and)
+    memset(R("kh", 0, 512), 0.0)
+    act(R("xt0", 1792, 1800), R("kh", 0, 8))
+    act(R("kh", 512, 1024), R("kh", 0, 512))
+    act(R("kh", 1024, 2048), R("kh", 0, 1024))
     ts(R("ci", 2, 3), R("ci", 0, 1), 4, A.arith_shift_right)
-    copy(P, R("ci", 0, 1))
     memset(tab(80), 0.5)
-    memset(tab(16, 16), 0.0)
-    copy(LANE, R("ci", 1, 2))
     copy(GRP, R("ci", 2, 3))
-    scan(tab(96), tab(80), tab(16), 256.0, A.mult, A.add)
+    memset(tab(0, 16), 2.0)
+    memset(tab(16, 16), 0.0)
+    scan(tab(96), tab(80), tab(80), 256.0, A.mult, A.max)
+    scan(tab(32, 16), tab(0, 16), tab(16, 16), 0.5, A.mult, A.add)
     ts(R("mk8"), R("jb", 0, 8), GRP, A.is_equal)
-    ts(HSC, LANE, 0.0, A.is_equal, -2.0 ** 23, A.mult)
-    ts(C112, P, 112.0, A.is_equal, -BIG, A.mult)
+    ts(LANE, GRP, -16.0, A.mult, P, A.add)
     tt(tab(80), R("mk8"), tab(96), A.mult)
+    ts(HSC, LANE, 0.0, A.is_equal, -2.0 ** 23, A.mult)
     red(IPW, tab(80))
+    ts(C112, P, 112.0, A.is_equal, -2.0 ** 30, A.mult)
+    ts(LM2, LANE, 2.0, A.subtract)
+    ts(CAB, LANE, 0.0, A.not_equal, 100.0, A.mult)
+    tt(NZ, LM2, GRP, A.not_equal)
+    ts(CAB, CAB, GRP, A.add, 2.0, A.add)
     ts(R("ijt"), R("ij"), IPW, A.mult)
     ts(R("iju"), R("ijt"), 128, A.bitwise_and)
+    copy(R("ou"), R("iu"))
     ts(R("bt"), R("iju"), HSC, A.mult)
     for h in range(2):
         for e in range(2):
@@ -249,25 +265,19 @@ def rank_program(g, core, T, topo):
     pick("up", 0, 256, "u", 128, R("ou"))
 
     def const_index():
+        ts(R("km"), R("r16", 0, 128), LANE, A.is_equal)
         for e in range(4):
-            ts(R("kx", e, 512, 4), R("r16", 0, 128), LANE, A.is_equal)
-        memset(R("vv"), 0.0)
-        quant("kx", 0, 128, R("kx"))
+            act(R("kx", e, 512, 4), R("km"))
+        for e in range(2):
+            act(R("lm", 128 * e, 128 * e + 128), R("km"))
+        op("a", lambda: g.scalar.activation(V(R("kp")), V(R("r16")), ACT.Sign), [R("kp")], [R("r16")])
         for k in range(2):
-            memset(R("mk%d" % k, 448, 456), -2.0 ** 59)
-        memset(R("sb", 448, 456), -2.0 ** 59)
-
-    def const_strength():
-        ts(R("lm"), R("r16"), LANE, A.is_equal)
-        ts(R("kp"), R("r16"), 0.0, A.not_equal)
-        ts(R("b8"), R("ib8"), LANE, A.add, 0.015625, A.mult)
+            memset(R("mk%d" % k, 448, 456), NONE)
+        memset(R("sb", 448, 456), NONE)
 
     def const_flags():
         memset(R("oz"), COLS)
         memset(R("an", 448, 512), 0.0)
-        ts(CAB, LANE, 0.0, A.not_equal, 100.0, A.mult)
-        tt(CAB, CAB, GRP, A.add)
-        ts(CAB, CAB, 2.0, A.add)
         for e in range(2):
             ts(R("kb", 512 * e + e, 512 * e + 512, 4), R("r16", 0, 128), CAB, A.is_equal)
         quant("kb", 0, 256, R("kb"))
@@ -276,53 +286,50 @@ def rank_program(g, core, T, topo):
         for b in range(4):
             act(R("ke", 512 * b + b, 512 * b + 512, 4), R("id"))
 
-    def const_lists():
-        memset(tab(0, 16), 2.0)
-        ts(R("ci", 3, 4), R("ci", 1, 2), 3, A.bitwise_and)
-        ts(LM2, LANE, 2.0, A.subtract)
-        scan(tab(32, 16), tab(0, 16), tab(16, 16), 0.5, A.mult, A.add)
+    def const_weights():
         copy(B4, R("ci", 3, 4))
-        tt(NZ, LM2, GRP, A.not_equal)
-        ts(tab(80, 16), R("r16", 0, 16), LANE, A.is_equal)
-        copy(tab(48, 16), tab(32, 16))
-        copy(tab(104), tab(32))
-        memset(tab(48, 2), 0.0)
-        memset(tab(58, 6), 0.0)
-        copy(tab(64, 16), tab(48, 16))
+        pw = tab(32)
+        if r:
+            pw = tab(104)
+            copy(pw, tab(32))
+        copy(tab(64, 16), tab(32, 16))
         for k in range(2):
             if r >> k & 1:
-                ts(tab(72 + k, 1), tab(56 + k, 1), -1.0, A.mult)
+                ts(tab(72 + k, 1), tab(40 + k, 1), -1.0, A.mult)
                 ts(tab(110 + k, 1), tab(38 + k, 1), -1.0, A.mult)
         memset(tab(64, 1), 2048.0)
-        tt(tab(96), R("mk8"), tab(104), A.mult)
+        tt(tab(96), R("mk8"), pw, A.mult)
         tt(tab(0, 16), tab(80, 16), tab(64, 16), A.mult)
         red(PWS, tab(96))
         red(WG0, tab(0, 16))
+
+    def const_lists():
         ts(S1, PWS, 4.0, A.mult, 256.0 * r, A.add)
         tt(WG0, WG0, NZ, A.mult)
         tt(S1, S1, B4, A.add)
         ts(S2, B4, 1024.0, A.add)
+        ts(GRP4, GRP, 4.0, A.mult)
         for e in range(4):
-            ts(cf(16 + e), GRP, 4.0, A.mult, float(e), A.add)
-        for e in range(4):
-            ts(R("ko", e, 512, 4), R("jq"), cf(16 + e), A.is_equal, WG0, A.mult)
+            ts(R("ko", e, 512, 4), R("jq", 128 * e, 128 * e + 128), GRP4, A.is_equal, WG0, A.mult)
         quant("ko", 0, 128, R("ko"))
 
     def const_wl():
-        tt(tab(0, 16), tab(80, 16), tab(48, 16), A.mult)
-        red(WG1, tab(0, 16))
+        tt(tab(0, 16), tab(80, 16), tab(32, 16), A.mult)
         ts(tab(96), R("jb", 0, 8), P, A.is_equal)
-        ts(WG1, WG1, NZ, A.mult, 0.25, A.mult)
+        ts(NZ, LANE, 0.0, A.not_equal, NZ, A.mult)
+        red(WG1, tab(0, 16))
         tt(tab(96), tab(96), tab(32), A.mult)
-        ts(R("id"), R("jb"), GRP, A.is_equal, WG1, A.mult)
+        ts(WG1, WG1, NZ, A.mult, 0.25, A.mult)
         red(PLB, tab(96))
+        ts(R("id"), R("jb"), GRP, A.is_equal, WG1, A.mult)
         diagonal()
-        quant("kw", 0, 512, R("ke"))
 
     chunks = ((0, CUT), (CUT, COLS))
+    ends = ((0, TAIL), (TAIL, COLS))
 
     def quant_state(k, c):
-        lo, hi = chunks[c][0], chunks[c][1] + 2 * c
+        lo, hi = (ends if k == ROUNDS else chunks)[c]
+        hi += 2 * c
         quant("x%d" % k, lo, hi, R("xt%d" % k, 4 * lo, 4 * hi))
 
     for c in range(2):
@@ -332,16 +339,26 @@ def rank_program(g, core, T, topo):
     for k in range(ROUNDS):
         X, state = "x%d" % k, "xt%d" % k
         C, L, TT, H, Z = ["%s%d" % (n, k) for n in "clthz"]
+        W, S = "wst%d" % k, "lst%d" % k
         last = k == ROUNDS - 1
+
+        def spread_strengths(c):
+            (lo, hi), bank = chunks[c], ("b4", "b7")[c]
+            mm(bank, "up", 128, X, lo, hi - lo)
+            act(R("sb", lo, hi), R(bank, 0, hi - lo), SMALL)
+
         for c, (lo, hi) in enumerate(chunks):
             mm("b%d" % (2 * c), "up", 0, X, lo, hi - lo)
             mm("b%d" % (2 * c + 1), "u", 0, X, lo, hi - lo)
             act(R("bc", lo, hi), R("b%d" % (2 * c), 0, hi - lo))
-        mm("b4", "up", 128, X, 0, COLS)
-        act(R("sb", 0, COLS), R("b4", 0, COLS), 2.0 ** -12)
+            if k:
+                spread_strengths(c)
+        if k == 0:
+            for c in range(2):
+                spread_strengths(c)
         for c, (lo, hi) in enumerate(chunks):
-            tt(R("dd", lo, hi), R("b%d" % (2 * c + 1), 0, hi - lo), R("bc", lo, hi), A.subtract)
-            ts(R("ft", c, c + 4 * (hi - lo) - 3, 4), R("dd", lo, hi), 0.0, A.is_le, BIG, A.mult)
+            n = hi - lo
+            tt(R("ft", c, c + 4 * n - 3, 4), R("b%d" % (2 * c + 1), 0, n), R("bc", lo, hi), A.is_le)
         quant("f", 0, CUT, R("ft"))
         banks = [["b5", "b6"], ["b7", "b0"]]
         for h in range(2):
@@ -353,48 +370,55 @@ def rank_program(g, core, T, topo):
             m, u = "mk%d" % h, "ru%d" % h
             for c, (lo, hi) in enumerate(chunks):
                 tt(R(m, lo, hi), R(banks[h][c], 0, hi - lo), R("sb", lo, hi), A.add)
-            scan(R(u, 0, 449), R(m, 0, 449), R(m, 0, 449), -2.0 ** 62, A.max, A.max)
-            i = R("ix", h, h + 1)
-            op("a", lambda: g.scalar.activation(V(R("jk%d" % h)), V(R(u, 0, COLS)), ACT.Sign, bias=V(R(u, COLS, COLS + 1)),
-                                                scale=-1.0, accum_out=V(i)), [R("jk%d" % h), i], [R(u, 0, 449)])
+            scan(R(u, 0, 449), R(m, 0, 449), R(m, 0, 449), LEAST, A.max, A.max)
+            i, j = R("ix", h, h + 1), R("jk%d" % h)
+            op("a", lambda: g.scalar.activation(V(j), V(R(u, 0, COLS)), ACT.Sign, bias=V(R(u, COLS, COLS + 1)), scale=-1.0,
+                                                accum_out=V(i)), [j, i], [R(u, 0, 449)])
         if k == 0:
-            const_strength()
+            quant("kx", 0, 128, R("kx"))
+            ts(R("b8"), R("ib8"), LANE, A.add, 0.015625, A.mult)
         for h in range(2):
             ts(R("xb", 8 * h, 8 * h + 8), R("mk8"), R("ix", h, h + 1), A.mult)
         ts(R("vv", 0, 64, 4), R("xb"), 402653184.0, A.add, -402653184.0, A.add)
         tt(R("vv", 1, 64, 4), R("xb"), R("vv", 0, 64, 4), A.subtract)
         quant("i", 0, 128, R("vv"))
         mm("b1", "kx", 0, "i", 0, 128)
+        if k == 0:
+            ts(R("ci", 3, 4), R("ci", 0, 1), 3, A.bitwise_and)
+            ts(tab(80, 16), R("r16", 0, 16), LANE, A.is_equal)
+            memset(tab(42, 6), 0.0)
         copy(R("of1"), R("b1", 0, 16))
         place = lambda o, n: n * (r ^ o)
-        W, S = "wst%d" % k, "lst%d" % k
-        pick(C, 0, 192, X, 450, R("of1", 4, 16))
-        scatter(0, lambda o: R(C + "_q", place(o, 64) - 64, place(o, 64)), lambda o: R(L + "_q", 64 * r, 64 * r + 64), "lc%d" % k)
+        pick_scales(C, 0, 192, X, 450, R("of1", 4, 16))
+        pick_codes(C, 0, 192, X, 450, R("of1", 4, 16))
         op("v", lambda: g.vector.tensor_tensor(V(R("gm")), V(R("sb", 0, 450)).indirect(V(R("of1"))), V(R("lm")), A.mult),
            [R("gm")], [R("sb", 0, 450), R("of1"), R("lm")])
         scan(R("gs"), R("kp"), R("gm"), 0.0, A.mult, A.add)
         copy(R(W), R("gs", 15, 256, 16))
-        scatter(1, lambda o: R(W, place(o, 4), place(o, 4) + 4), lambda o: R(S, STRONG[r], STRONG[r] + 4), "lt%d" % k)
-        scatter(2, lambda o: R(C + "_s", place(o, 64) - 64, place(o, 64)), lambda o: R(L + "_s", 64 * r, 64 * r + 64), "lp%d" % k)
+        scatter(0, lambda o: R(C + "_q", place(o, 64) - 64, place(o, 64)), R(L + "_q", 64 * r, 64 * r + 64), "lc%d" % k)
+        scatter(1, lambda o: R(W, place(o, 4), place(o, 4) + 4), R(S, STRONG[r], STRONG[r] + 4), "lt%d" % k)
+        scatter(2, lambda o: R(C + "_s", place(o, 64) - 64, place(o, 64)), R(L + "_s", 64 * r, 64 * r + 64), "lp%d" % k)
         if k == 0:
-            act(R("kb"), R("kh", 0, 1024), 0.0)
+            iota(R("ke", 0, 1024), [[0, 1024]], 0, 0)
+            iota(R("jq"), [[-1, 4], [1, 32], [0, 4]], 0, 0)
         pick(L, 64 * r, 64 * r + 64, X, 450, R("of1", 0, 4))
         copy(R(S, STRONG[r], STRONG[r] + 4), R(W, 0, 4))
+        for c, (lo, hi) in enumerate(chunks):
+            act(R("ww", lo, hi), R("ft", c, c + 4 * (hi - lo) - 3, 4), -1.0, 1.0)
         if k == 0:
+            act(R("ke", 1024, 2048), R("kh", 0, 1024), 0.0)
+            ts(R("id"), R("jb"), P, A.is_equal)
             const_flags()
         pick(TT, 64, 128, X, 450, R("oz"))
-        ts(R("ww"), R("dd"), 0.0, A.is_gt)
         for c, (lo, hi) in enumerate(chunks):
             mm("b%d" % (2 + c), "kb", 128 * c, "f", 0, hi - lo)
             tt(R("an", lo, hi), R("ww", lo, hi), R("b%d" % (2 + c), 0, hi - lo), A.is_gt)
         quant("a", 0, 128, R("an"))
         if k == 0:
-            ts(R("id"), R("jb"), P, A.is_equal)
-            memset(R("hh"), 0.0)
+            memset(R("hh", 256, 512), 0.0)
             memset(R("yy", 1024, 1040), 0.0)
-            act(R("ke"), R("kh"), 0.0)
-            diagonal()
         if last:
+            quant("v", 0, 128, R("vt"))
             const_wl()
         tt(R("sel"), R(S, 8, 16), R(S, 0, 8), A.is_gt)
         tt(R("mx8"), R(S, 8, 16), R(S, 0, 8), A.max)
@@ -417,8 +441,9 @@ def rank_program(g, core, T, topo):
         spread(True, R(H + "_q", 0, 64), lambda o: R(Z + "_q", slot(o), slot(o) + 64), "hc%d" % k)
         spread(False, R(H + "_s", 0, 64), lambda o: R(Z + "_s", slot(o), slot(o) + 64), "hp%d" % k)
         if k == 0:
+            diagonal()
+            const_weights()
             quant("ke", 0, 512, R("ke"))
-            quant("v", 0, 128, R("vt"))
         memset(R("xt%d" % (k + 1), 1792, 1800), 0.0)
         ob = ["b1", "b2", "b3", "b4"]
         for b in range(4):
@@ -429,6 +454,7 @@ def rank_program(g, core, T, topo):
         mm("b4", "ko", 0, "a", 0, 128)
         ts(R("ofx"), R("b4", 0, 112), S1, A.add, S2, A.min)
         if last:
+            quant("kw", 0, 512, R("ke"))
             for b in range(4):
                 mm(ob[b], "kw", 128 * b, "a", 0, 128)
                 o, i = R("wlb", b, COLS, 4), R(ob[b], 0, 112)
@@ -441,17 +467,18 @@ def rank_program(g, core, T, topo):
                 copy(o, i)
             else:
                 act(o, i)
-        for c, (lo, hi) in enumerate(chunks):
+        for c, (lo, hi) in enumerate(ends if last else chunks):
             o, i, f = R("xt%d" % (k + 1), 4 * lo, 4 * hi), R(state, 4 * lo, 4 * hi), R("ofx", lo // 4, hi // 4)
             op("v", lambda: g.vector.tensor_tensor(V(o), V(R("yy")).indirect(V(f)), V(i), A.add), [o], [R("yy"), f, i])
             quant_state(k + 1, c)
 
-    for c, (lo, hi) in enumerate(chunks):
+    for c, (lo, hi) in enumerate(ends):
         dma("s", "stored", T.oc[:, 4 * lo:4 * hi], V(R("x2_q", lo, hi)).bitcast(dt.uint8), [], [R("x2_q", lo, hi)])
         mm("b%d" % c, "v", 0, "x2", lo, hi - lo)
         act(R("yo", lo, hi), R("b%d" % c, 0, hi - lo))
+        if c:
+            for q in range(4):
+                dma("s", "stored", T.osc[4 * q:4 * q + 4, :], T.x2_s[32 * q:32 * q + 4, 0:COLS], [], [R("x2_s", 0, COLS)])
         dma("s", "stored", T.y[:, lo:hi], V(R("yo", lo, hi)), [], [R("yo", lo, hi)])
-    for q in range(4):
-        dma("a", "stored", T.osc[4 * q:4 * q + 4, :], T.x2_s[32 * q:32 * q + 4, 0:COLS], [], [R("x2_s", 0, COLS)])
     for s in sorted(total):
         wait("g", (s, total[s]))

from concourse.bass import DstId, RemoteDMATransfer
from concourse.mybir import dt, AluOpType, AxisListType, ActivationFunctionType

F8, U8, U16, I32, F32, BF = "float8_e4m3fn_x4", "uint8", "uint16", "int32", "float32", "bfloat16"
ROUNDS, COLS = 2, 448
CUT, TAIL = 256, 320
SMALL, NONE, LEAST = 2.0 ** -42, -2.0 ** 29, -2.0 ** 34
SCRATCH = {}


def buf(name, n, dtype, where="sbuf"):
    SCRATCH[name] = (where, [128, n], dtype)


for _k in range(3):
    buf("xt%d" % _k, 1800, BF)
    buf("x%d_q" % _k, 450, F8)
    buf("x%d_s" % _k, 450, U8)
for _k in range(2):
    for _n, _w in (("c", 192), ("l", 256), ("t", 128), ("h", 128), ("z", 192)):
        buf("%s%d_q" % (_n, _k), _w, F8)
        buf("%s%d_s" % (_n, _k), _w, U8)
    buf("wst%d" % _k, 16, F32)
    buf("lst%d" % _k, 16, F32)
    buf("mk%d" % _k, 456, F32)
    buf("ru%d" % _k, 456, F32)
    buf("jk%d" % _k, 448, BF)
for _n, _w in (("u", 128), ("v", 128), ("up", 256), ("w", 512), ("f", CUT), ("i", 128), ("a", 128),
               ("kh", 512), ("kx", 128), ("kb", 256), ("ko", 128), ("ke", 512), ("kw", 512)):
    buf(_n + "_q", _w, F8)
    buf(_n + "_s", _w, U8)
for _n, _w in (("ut", 512), ("vt", 512), ("ft", 4 * CUT), ("id", 128), ("km", 128), ("vv", 512), ("hh", 512), ("yy", 1040),
               ("ww", 448), ("an", 512), ("kh", 2048), ("kx", 512), ("kb", 1024), ("ko", 512), ("ke", 2048),
               ("jb", 128), ("jq", 512), ("r16", 256), ("bt", 128)):
    buf(_n, _w, BF)
for _n, _w in (("bc", 448), ("sb", 456), ("ix", 2), ("xb", 16), ("gm", 256), ("gs", 256), ("sel", 8), ("mx8", 8), ("gg", 8),
               ("f4", 4), ("e4", 4), ("o4", 4), ("yo", 448), ("wlb", 448), ("cf", 32), ("lm", 256), ("kp", 256), ("b8", 8),
               ("ib8", 8), ("mk8", 8), ("tab", 112)):
    buf(_n, _w, F32)
for _n, _w in (("ci", 8), ("ij", 128), ("ijt", 128), ("iju", 128), ("iu", 16)):
    buf(_n, _w, I32)
for _n, _w in (("ou", 16), ("oz", 4), ("of1", 16), ("oft", 4), ("ofx", 112)):
    buf(_n, _w, U16)
PSUM = ["b%d" % _k for _k in range(8)]
for _n in PSUM:
    buf(_n, 512, F32, "psum")
SEMAPHORES = (["v", "a", "t", "gp", "sent", "stored", "dx0", "dx1", "du", "dv", "dwc", "dws"]
              + ["%s%d" % (n, k) for n in ("lc", "lp", "lt", "hc", "hp") for k in range(2)])


def rank_program(g, core, T, topo):
    r = T.rank_of(core)
    if r is None:
        return
    A, ACT = AluOpType, ActivationFunctionType
    queues = {"v": g.vector, "a": g.scalar, "t": g.tensor, "g": g, "s": g.sync}
    own_sem = {"v": "v", "a": "a", "t": "t", "g": "gp"}
    total, know, snap, acc = {}, {q: {} for q in queues}, {}, {}

    def R(name, lo=0, hi=None, step=1):
        return (name, lo, SCRATCH[name][1][1] if hi is None else hi, step)

    def V(x):
        return T[x[0]][:, x[1]:x[2]] if x[3] == 1 else T[x[0]][:, x[1]:x[2]:x[3]]

    def hit(p, q):
        if max(p[1], q[1]) >= min(p[2], q[2]):
            return False
        return p[3] != q[3] or (p[1] - q[1]) % p[3] == 0

    def wait(q, tok):
        sem, val = tok
        if know[q].get(sem, 0) >= val:
            return
        queues[q].wait_ge(T.sem[sem], val)
        for s, x in list(snap.get(tok, {}).items()) + [tok]:
            know[q][s] = max(know[q].get(s, 0), x)

    def deps(q, lane, reads, writes):
        need = set()
        for reg, isw in [(x, False) for x in reads] + [(x, True) for x in writes]:
            for old, oldw, oldlane, tok in acc.get(reg[0], []):
                if reg[0] in PSUM:
                    if oldlane == lane:
                        continue
                elif not (isw or oldw) or not hit(old, reg):
                    continue
                need.add(tok)
        for tok in sorted(need, key=lambda x: -x[1]):
            wait(q, tok)

    def note(lane, tok, reads, writes):
        for reg, isw in [(x, False) for x in reads] + [(x, True) for x in writes]:
            acc.setdefault(reg[0], []).append((reg, isw, lane, tok))

    def op(q, fn, writes, reads):
        deps(q, q, reads, writes)
        s = own_sem[q]
        total[s] = total.get(s, 0) + 1
        tok = (s, total[s])
        fn().then_inc(T.sem[s], 1)
        snap[tok] = dict(know[q])
        note(q, tok, reads, writes)

    def dma(q, sem, out, in_, writes, reads):
        deps(q, "dma", reads, writes)
        total[sem] = total.get(sem, 0) + 16
        queues[q].dma_start(out, in_).then_inc(T.sem[sem], 16)
        tok = (sem, total[sem])
        snap[tok] = dict(know[q])
        note("dma", tok, reads, writes)

    def memset(o, c):
        op("v", lambda: g.vector.memset(V(o), c), [o], [])

    def copy(o, i):
        op("v", lambda: g.vector.tensor_copy(V(o), V(i)), [o], [i])

    def tt(o, i, j, f):
        op("v", lambda: g.vector.tensor_tensor(V(o), V(i), V(j), f), [o], [i, j])

    def ts(o, i, s1, f1, s2=None, f2=None):
        v = lambda s: V(s) if isinstance(s, tuple) else s
        rd = [i] + [s for s in (s1, s2) if isinstance(s, tuple)]
        if f2 is None:
            op("v", lambda: g.vector.tensor_scalar(V(o), V(i), v(s1), None, f1), [o], rd)
        else:
            op("v", lambda: g.vector.tensor_scalar(V(o), V(i), v(s1), v(s2), f1, f2), [o], rd)

    def red(o, i):
        op("v", lambda: g.vector.tensor_reduce(V(o), V(i), AxisListType.X, A.add), [o], [i])

    def scan(o, i, j, init, f1, f2):
        op("v", lambda: g.vector.tensor_tensor_scan(V(o), V(i), V(j), init, f1, f2), [o], [i, j])

    def act(o, i, scale=1.0, bias=0.0):
        op("a", lambda: g.scalar.activation(V(o), V(i), ACT.Copy, bias=bias, scale=scale), [o], [i])

    def iota(o, pattern, base, ch):
        if SCRATCH[o[0]][2] == I32:
            op("g", lambda: g.iota(V(o), pattern, base, ch), [o], [])
        else:
            op("g", lambda: g.iota(V(o), pattern, base, ch, allow_small_or_imprecise_dtypes=True), [o], [])

    def quant(m, lo, hi, i):
        q, s = R(m + "_q", lo, hi), R(m + "_s", lo, hi)
        op("v", lambda: g.vector.quantize_mx(V(q), V(s), V(i)), [q, s], [i])

    def mm(bank, w, wlo, m, mlo, n):
        o = R(bank, 0, n)
        i = [R(w + "_q", wlo, wlo + 128), R(w + "_s", wlo, wlo + 128), R(m + "_q", mlo, mlo + n), R(m + "_s", mlo, mlo + n)]
        op("t", lambda: g.tensor.matmul_mx(V(o), V(i[0]), V(i[1]), V(i[2]), V(i[3]), True, True), [o], i)

    def pick_codes(o, lo, hi, w, wide, f):
        q, wq = R(o + "_q", lo, hi), R(w + "_q", 0, wide)
        op("v", lambda: g.vector.tensor_copy(V(q).bitcast(dt.uint32), V(wq).bitcast(dt.uint32).indirect(V(f))), [q], [wq, f])

    def pick_scales(o, lo, hi, w, wide, f):
        s, wp = R(o + "_s", lo, hi), R(w + "_s", 0, wide)
        op("a", lambda: g.scalar.activation(V(s), V(wp).indirect(V(f)), ACT.Copy), [s], [wp, f])

    def pick(*a):
        pick_codes(*a)
        pick_scales(*a)

    def cf(k):
        return R("cf", k, k + 1)

    def tab(k, n=8):
        return R("tab", k, k + n)

    others = [r ^ d for d in (1, 2, 3)]
    eng = topo.engines(core, T.cores[others[0]])
    bits = lambda es: sum(1 << e for e in es)
    half, quarter = len(eng) // 2, len(eng) // 4
    one, two = eng[:half], eng[half:]
    cut = lambda es: [es[:quarter], es[quarter:]]
    split = [[one] + cut(two), [cut(one)[0], two, cut(one)[1]], cut(one) + [two]]

    def dest(o):
        rid, pid, _ = topo.addr(T.cores[o])
        return DstId(rid=rid, pnc=pid)

    def view(x, codes):
        return V(x).bitcast(dt.uint8) if codes else V(x)

    def scatter(kind, src, dst, sem):
        deps("g", "rem", [src(o) for o in others], [])
        g.remote_dma_fused([RemoteDMATransfer(dst_ids=[dest(o)], dma_engine_mask=bits(split[kind][d]), remote_sem=T.sem[sem],
                                              src=view(src(o), kind == 0), dst=view(dst, kind == 0))
                            for d, o in enumerate(others)], local_sem=T.sem.sent)
        total["sent"] = total.get("sent", 0) + len(eng)

    def spread(codes, src, dst, sem):
        deps("g", "rem", [src], [])
        g.remote_dma_fused([RemoteDMATransfer(dst_ids=[dest(o) for o in others], dma_engine_mask=bits(eng), remote_sem=T.sem[sem],
                                              srcs=[view(src, codes)], dsts=[view(dst(o), codes) for o in others])],
                           local_sem=T.sem.sent)
        total["sent"] = total.get("sent", 0) + len(eng)

    STRONG = [0, 8, 4, 12]
    for k in range(ROUNDS):
        for sem, val, regs in (("lc%d", len(eng), [R("l%d_q" % k, 64 * o, 64 * o + 64) for o in others]),
                               ("lp%d", len(eng), [R("l%d_s" % k, 64 * o, 64 * o + 64) for o in others]),
                               ("lt%d", len(eng), [R("lst%d" % k, STRONG[o], STRONG[o] + 4) for o in others]),
                               ("hc%d", 3 * len(eng), [R("z%d_q" % k)]),
                               ("hp%d", 3 * len(eng), [R("z%d_s" % k)])):
            total[sem % k] = val
            note("rem", (sem % k, val), [], regs)

    dma("s", "dx0", T.xt0[:, 0:4 * CUT], T.x[:, 0:4 * CUT], [R("xt0", 0, 4 * CUT)], [])
    dma("a", "du", V(R("ut")), T.u[:, :], [R("ut")], [])
    dma("s", "dx1", T.xt0[:, 4 * CUT:1792], T.x[:, 4 * CUT:1792], [R("xt0", 4 * CUT, 1792)], [])
    wait("s", ("dx1", 16))
    dma("s", "dwc", V(R("w_q")).bitcast(dt.uint8), T.wc[:, :], [R("w_q")], [])
    dma("s", "dws", V(R("w_s")), T.ws[:, :], [R("w_s")], [])
    dma("s", "dv", V(R("vt")), T.v[:, :], [R("vt")], [])

    P, LANE, GRP, B4, IPW, HSC, C112, PWS, S1, S2, WG0, WG1, PLB, NZ, CAB, LM2, GRP4 = [cf(k) for k in range(17)]
    iota(R("ci", 0, 1), [[0, 1]], 0, 1)
    iota(P, [[0, 1]], 0, 1)
    iota(R("jb"), [[1, 128]], 0, 0)
    iota(R("iu", 0, 8), [[16, 8]], 1, 0)
    iota(R("iu", 8, 16), [[0, 8]], 15, 0)
    iota(R("ij"), [[-64, 2], [1, 64]] if r & 1 else [[64, 2], [1, 64]], 64 * (r & 1), 0)
    iota(R("ft"), [[0, 4 * CUT]], 0, 0)
    iota(R("r16"), [[0, 16], [1, 16]], 0, 0)
    iota(R("ib8"), [[128, 2], [16, 4]], 0, 0)
    iota(R("vv"), [[0, 512]], 0, 0)
    iota(R("kb"), [[0, 1024]], 0, 0)

    memset(R("kh", 0, 512), 0.0)
    act(R("xt0", 1792, 1800), R("kh", 0, 8))
    act(R("kh", 512, 1024), R("kh", 0, 512))
    act(R("kh", 1024, 2048), R("kh", 0, 1024))
    ts(R("ci", 2, 3), R("ci", 0, 1), 4, A.arith_shift_right)
    memset(tab(80), 0.5)
    copy(GRP, R("ci", 2, 3))
    memset(tab(0, 16), 2.0)
    memset(tab(16, 16), 0.0)
    scan(tab(96), tab(80), tab(80), 256.0, A.mult, A.max)
    scan(tab(32, 16), tab(0, 16), tab(16, 16), 0.5, A.mult, A.add)
    ts(R("mk8"), R("jb", 0, 8), GRP, A.is_equal)
    ts(LANE, GRP, -16.0, A.mult, P, A.add)
    tt(tab(80), R("mk8"), tab(96), A.mult)
    ts(HSC, LANE, 0.0, A.is_equal, -2.0 ** 23, A.mult)
    red(IPW, tab(80))
    ts(C112, P, 112.0, A.is_equal, -2.0 ** 30, A.mult)
    ts(LM2, LANE, 2.0, A.subtract)
    ts(CAB, LANE, 0.0, A.not_equal, 100.0, A.mult)
    tt(NZ, LM2, GRP, A.not_equal)
    ts(CAB, CAB, GRP, A.add, 2.0, A.add)
    ts(R("ijt"), R("ij"), IPW, A.mult)
    ts(R("iju"), R("ijt"), 128, A.bitwise_and)
    copy(R("ou"), R("iu"))
    ts(R("bt"), R("iju"), HSC, A.mult)
    for h in range(2):
        for e in range(2):
            o = R("kh", 1024 * h + 513 * e, 1024 * h + 512 * e + 512, 4)
            if h ^ r >> 1:
                ts(o, R("bt"), C112, A.min)
            else:
                act(o, R("bt"))
    quant("u", 0, 128, R("ut"))
    pick("up", 0, 256, "u", 128, R("ou"))

    def const_index():
        ts(R("km"), R("r16", 0, 128), LANE, A.is_equal)
        for e in range(4):
            act(R("kx", e, 512, 4), R("km"))
        for e in range(2):
            act(R("lm", 128 * e, 128 * e + 128), R("km"))
        op("a", lambda: g.scalar.activation(V(R("kp")), V(R("r16")), ACT.Sign), [R("kp")], [R("r16")])
        for k in range(2):
            memset(R("mk%d" % k, 448, 456), NONE)
        memset(R("sb", 448, 456), NONE)

    def const_flags():
        memset(R("oz"), COLS)
        memset(R("an", 448, 512), 0.0)
        for e in range(2):
            ts(R("kb", 512 * e + e, 512 * e + 512, 4), R("r16", 0, 128), CAB, A.is_equal)
        quant("kb", 0, 256, R("kb"))

    def diagonal():
        for b in range(4):
            act(R("ke", 512 * b + b, 512 * b + 512, 4), R("id"))

    def const_weights():
        copy(B4, R("ci", 3, 4))
        pw = tab(32)
        if r:
            pw = tab(104)
            copy(pw, tab(32))
        copy(tab(64, 16), tab(32, 16))
        for k in range(2):
            if r >> k & 1:
                ts(tab(72 + k, 1), tab(40 + k, 1), -1.0, A.mult)
                ts(tab(110 + k, 1), tab(38 + k, 1), -1.0, A.mult)
        memset(tab(64, 1), 2048.0)
        tt(tab(96), R("mk8"), pw, A.mult)
        tt(tab(0, 16), tab(80, 16), tab(64, 16), A.mult)
        red(PWS, tab(96))
        red(WG0, tab(0, 16))

    def const_lists():
        ts(S1, PWS, 4.0, A.mult, 256.0 * r, A.add)
        tt(WG0, WG0, NZ, A.mult)
        tt(S1, S1, B4, A.add)
        ts(S2, B4, 1024.0, A.add)
        ts(GRP4, GRP, 4.0, A.mult)
        for e in range(4):
            ts(R("ko", e, 512, 4), R("jq", 128 * e, 128 * e + 128), GRP4, A.is_equal, WG0, A.mult)
        quant("ko", 0, 128, R("ko"))

    def const_wl():
        tt(tab(0, 16), tab(80, 16), tab(32, 16), A.mult)
        ts(tab(96), R("jb", 0, 8), P, A.is_equal)
        ts(NZ, LANE, 0.0, A.not_equal, NZ, A.mult)
        red(WG1, tab(0, 16))
        tt(tab(96), tab(96), tab(32), A.mult)
        ts(WG1, WG1, NZ, A.mult, 0.25, A.mult)
        red(PLB, tab(96))
        ts(R("id"), R("jb"), GRP, A.is_equal, WG1, A.mult)
        diagonal()

    chunks = ((0, CUT), (CUT, COLS))
    ends = ((0, TAIL), (TAIL, COLS))

    def quant_state(k, c):
        lo, hi = (ends if k == ROUNDS else chunks)[c]
        hi += 2 * c
        quant("x%d" % k, lo, hi, R("xt%d" % k, 4 * lo, 4 * hi))

    for c in range(2):
        quant_state(0, c)
    quant("kh", 0, 512, R("kh"))

    for k in range(ROUNDS):
        X, state = "x%d" % k, "xt%d" % k
        C, L, TT, H, Z = ["%s%d" % (n, k) for n in "clthz"]
        W, S = "wst%d" % k, "lst%d" % k
        last = k == ROUNDS - 1

        def spread_strengths(c):
            (lo, hi), bank = chunks[c], ("b4", "b7")[c]
            mm(bank, "up", 128, X, lo, hi - lo)
            act(R("sb", lo, hi), R(bank, 0, hi - lo), SMALL)

        for c, (lo, hi) in enumerate(chunks):
            mm("b%d" % (2 * c), "up", 0, X, lo, hi - lo)
            mm("b%d" % (2 * c + 1), "u", 0, X, lo, hi - lo)
            act(R("bc", lo, hi), R("b%d" % (2 * c), 0, hi - lo))
            if k:
                spread_strengths(c)
        if k == 0:
            for c in range(2):
                spread_strengths(c)
        for c, (lo, hi) in enumerate(chunks):
            n = hi - lo
            tt(R("ft", c, c + 4 * n - 3, 4), R("b%d" % (2 * c + 1), 0, n), R("bc", lo, hi), A.is_le)
        quant("f", 0, CUT, R("ft"))
        banks = [["b5", "b6"], ["b7", "b0"]]
        for h in range(2):
            for c, (lo, hi) in enumerate(chunks):
                mm(banks[h][c], "kh", 128 * (2 * h + c), "f", 0, hi - lo)
        if k == 0:
            const_index()
        for h in range(2):
            m, u = "mk%d" % h, "ru%d" % h
            for c, (lo, hi) in enumerate(chunks):
                tt(R(m, lo, hi), R(banks[h][c], 0, hi - lo), R("sb", lo, hi), A.add)
            scan(R(u, 0, 449), R(m, 0, 449), R(m, 0, 449), LEAST, A.max, A.max)
            i, j = R("ix", h, h + 1), R("jk%d" % h)
            op("a", lambda: g.scalar.activation(V(j), V(R(u, 0, COLS)), ACT.Sign, bias=V(R(u, COLS, COLS + 1)), scale=-1.0,
                                                accum_out=V(i)), [j, i], [R(u, 0, 449)])
        if k == 0:
            quant("kx", 0, 128, R("kx"))
            ts(R("b8"), R("ib8"), LANE, A.add, 0.015625, A.mult)
        for h in range(2):
            ts(R("xb", 8 * h, 8 * h + 8), R("mk8"), R("ix", h, h + 1), A.mult)
        ts(R("vv", 0, 64, 4), R("xb"), 402653184.0, A.add, -402653184.0, A.add)
        tt(R("vv", 1, 64, 4), R("xb"), R("vv", 0, 64, 4), A.subtract)
        quant("i", 0, 128, R("vv"))
        mm("b1", "kx", 0, "i", 0, 128)
        if k == 0:
            ts(R("ci", 3, 4), R("ci", 0, 1), 3, A.bitwise_and)
            ts(tab(80, 16), R("r16", 0, 16), LANE, A.is_equal)
            memset(tab(42, 6), 0.0)
        copy(R("of1"), R("b1", 0, 16))
        place = lambda o, n: n * (r ^ o)
        pick_scales(C, 0, 192, X, 450, R("of1", 4, 16))
        pick_codes(C, 0, 192, X, 450, R("of1", 4, 16))
        op("v", lambda: g.vector.tensor_tensor(V(R("gm")), V(R("sb", 0, 450)).indirect(V(R("of1"))), V(R("lm")), A.mult),
           [R("gm")], [R("sb", 0, 450), R("of1"), R("lm")])
        scan(R("gs"), R("kp"), R("gm"), 0.0, A.mult, A.add)
        copy(R(W), R("gs", 15, 256, 16))
        scatter(0, lambda o: R(C + "_q", place(o, 64) - 64, place(o, 64)), R(L + "_q", 64 * r, 64 * r + 64), "lc%d" % k)
        scatter(1, lambda o: R(W, place(o, 4), place(o, 4) + 4), R(S, STRONG[r], STRONG[r] + 4), "lt%d" % k)
        scatter(2, lambda o: R(C + "_s", place(o, 64) - 64, place(o, 64)), R(L + "_s", 64 * r, 64 * r + 64), "lp%d" % k)
        if k == 0:
            iota(R("ke", 0, 1024), [[0, 1024]], 0, 0)
            iota(R("jq"), [[-1, 4], [1, 32], [0, 4]], 0, 0)
        pick(L, 64 * r, 64 * r + 64, X, 450, R("of1", 0, 4))
        copy(R(S, STRONG[r], STRONG[r] + 4), R(W, 0, 4))
        for c, (lo, hi) in enumerate(chunks):
            act(R("ww", lo, hi), R("ft", c, c + 4 * (hi - lo) - 3, 4), -1.0, 1.0)
        if k == 0:
            act(R("ke", 1024, 2048), R("kh", 0, 1024), 0.0)
            ts(R("id"), R("jb"), P, A.is_equal)
            const_flags()
        pick(TT, 64, 128, X, 450, R("oz"))
        for c, (lo, hi) in enumerate(chunks):
            mm("b%d" % (2 + c), "kb", 128 * c, "f", 0, hi - lo)
            tt(R("an", lo, hi), R("ww", lo, hi), R("b%d" % (2 + c), 0, hi - lo), A.is_gt)
        quant("a", 0, 128, R("an"))
        if k == 0:
            memset(R("hh", 256, 512), 0.0)
            memset(R("yy", 1024, 1040), 0.0)
        if last:
            quant("v", 0, 128, R("vt"))
            const_wl()
        tt(R("sel"), R(S, 8, 16), R(S, 0, 8), A.is_gt)
        tt(R("mx8"), R(S, 8, 16), R(S, 0, 8), A.max)
        tt(R("gg"), R("sel"), R("b8"), A.add)
        tt(R("f4"), R("mx8", 4, 8), R("mx8", 0, 4), A.is_gt)
        tt(R("e4"), R("f4"), R("gg", 4, 8), A.mult)
        tt(R("o4"), R("e4"), R("gg", 0, 4), A.max)
        ts(R("oft"), R("o4"), 64.0, A.mult)
        pick(TT, 0, 64, L, 256, R("oft"))
        hb = ["b5", "b6", "b7", "b0"]
        for b in range(4):
            mm(hb[b], "w", 128 * b, TT, 0, 128)
            o, i = R("hh", b, 256, 4), R(hb[b], 0, 64)
            if b % 2:
                ts(o, i, 0.03125, A.mult)
            else:
                act(o, i, 0.03125)
        quant(H, 0, 128, R("hh"))
        slot = lambda o: 64 * ((r ^ o) - 1)
        spread(True, R(H + "_q", 0, 64), lambda o: R(Z + "_q", slot(o), slot(o) + 64), "hc%d" % k)
        spread(False, R(H + "_s", 0, 64), lambda o: R(Z + "_s", slot(o), slot(o) + 64), "hp%d" % k)
        if k == 0:
            diagonal()
            const_weights()
            quant("ke", 0, 512, R("ke"))
        memset(R("xt%d" % (k + 1), 1792, 1800), 0.0)
        ob = ["b1", "b2", "b3", "b4"]
        for b in range(4):
            mm(ob[b], "ke", 128 * b, H, 0, 128)
            act(R("yy", b, 256, 4), R(ob[b], 0, 64))
        if k == 0:
            const_lists()
        mm("b4", "ko", 0, "a", 0, 128)
        ts(R("ofx"), R("b4", 0, 112), S1, A.add, S2, A.min)
        if last:
            quant("kw", 0, 512, R("ke"))
            for b in range(4):
                mm(ob[b], "kw", 128 * b, "a", 0, 128)
                o, i = R("wlb", b, COLS, 4), R(ob[b], 0, 112)
                op("a", lambda: g.scalar.activation(V(o), V(i), ACT.Identity, bias=V(PLB)), [o], [i, PLB])
            dma("s", "stored", T.wl[:, :], T.wlb[0:8, 0:COLS], [], [R("wlb")])
        for b in range(4):
            mm(hb[b], "ke", 128 * b, Z, 0, 192)
            o, i = R("yy", 256 + b, 1024, 4), R(hb[b], 0, 192)
            if b % 2:
                copy(o, i)
            else:
                act(o, i)
        for c, (lo, hi) in enumerate(ends if last else chunks):
            o, i, f = R("xt%d" % (k + 1), 4 * lo, 4 * hi), R(state, 4 * lo, 4 * hi), R("ofx", lo // 4, hi // 4)
            op("v", lambda: g.vector.tensor_tensor(V(o), V(R("yy")).indirect(V(f)), V(i), A.add), [o], [R("yy"), f, i])
            quant_state(k + 1, c)

    for c, (lo, hi) in enumerate(ends):
        dma("s", "stored", T.oc[:, 4 * lo:4 * hi], V(R("x2_q", lo, hi)).bitcast(dt.uint8), [], [R("x2_q", lo, hi)])
        mm("b%d" % c, "v", 0, "x2", lo, hi - lo)
        act(R("yo", lo, hi), R("b%d" % c, 0, hi - lo))
        if c:
            for q in range(4):
                dma("s", "stored", T.osc[4 * q:4 * q + 4, :], T.x2_s[32 * q:32 * q + 4, 0:COLS], [], [R("x2_s", 0, COLS)])
        dma("s", "stored", T.y[:, lo:hi], V(R("yo", lo, hi)), [], [R("yo", lo, hi)])
    for s in sorted(total):
        wait("g", (s, total[s]))
